import numpy as np, ml_dtypes
CORES = [76,84,92,100,108,116,124]
N = 7
F = 128
def setup_inputs(rng):
    m = (rng.standard_normal((N, 128, 128), dtype=np.float32) / 11).astype(ml_dtypes.bfloat16)
    return {"m": m, "mt": m.transpose(0, 2, 1).copy(), "x": rng.standard_normal((N, 128, F), dtype=np.float32).astype(ml_dtypes.bfloat16)}
def setup_inputs_big(rng):
    d = setup_inputs(rng)
    for k in ("x",): d[k] = (d[k].astype(np.float32) * 1048576.0).astype(d[k].dtype)
    return d
def setup_inputs_small(rng):
    d = setup_inputs(rng)
    for k in ("x",): d[k] = (d[k].astype(np.float32) * (1 / 1048576.0)).astype(d[k].dtype)
    return d
def setup_inputs_apart(rng):
    d = setup_inputs(rng)
    f = (10.0 ** rng.permutation(np.linspace(-1.5, 1.5, N))).astype(np.float32).reshape(N, 1, 1)
    for k in ("x",): d[k] = (d[k].astype(np.float32) * f).astype(d[k].dtype)
    return d
def reference(m, mt, x):
    M, X = m.astype(np.float64), x.astype(np.float64)
    y = np.zeros((N, 128, F)); p = X[0]
    for r in range(N):
        p = M[r].T @ p
        y[r] = p
    return {"y": y.astype(ml_dtypes.bfloat16)}

from concourse.bass import DstId, RemoteDMATransfer

N_CORES = 128
E_ON = 8
E_OFF = 8
BF = "bfloat16"

_SBUF = ["own", "sx", "in0", "inx", "inp", "in1", "in2", "in3", "in4", "in5", "prel"] + ["t%d" % i for i in range(6)]
SCRATCH = {"dsend": ("dram", [2, 128, 128], BF), "drel": ("dram", [128, 128], BF)}
for _n in _SBUF:
    SCRATCH[_n] = ("sbuf", [128, 128], BF)
for _i in range(6):
    SCRATCH["ps%d" % _i] = ("psum", [128, 512], "float32")

SEMAPHORES = (["ldd", "lds", "rel", "relp", "sent", "st", "a0", "ax", "ap", "a1", "a2", "a3", "a4", "a5"]
              + ["mm%d" % i for i in range(6)] + ["cp%d" % i for i in range(6)])

STAGE = {1: "mt", 2: "m", 3: "mt", 4: "m", 5: "mt"}
PLAN = {
    0: [("own", "sx")],
    1: [("own", "inp")],
    2: [("in1", "own"), ("t0", "inp")],
    3: [("in2", "in1"), ("t0", "own"), ("t1", "inp")],
    4: [("in3", "own"), ("in2", "in1"), ("t1", "t0"), ("t2", "inp")],
    5: [("in4", "in3"), ("in1", "in2"), ("in0", "inx"), ("t0", "own"), ("t1", "t2"), ("t3", "t4")],
    6: [("in4", "in3"), ("in5", "own"), ("in1", "in2"), ("t0", "t1"), ("t2", "inp"), ("t3", "t4")],
}
ARR = {"in0": "a0", "inx": "ax", "inp": "ap", "in1": "a1", "in2": "a2", "in3": "a3", "in4": "a4", "in5": "a5"}


def _bits(mask, n, skip=0):
    out, seen, b = 0, 0, 0
    while mask >> b:
        if (mask >> b) & 1:
            if skip <= seen < skip + n:
                out |= 1 << b
            seen += 1
        b += 1
    return out


def _routes(T, topo):
    cores = T.cores
    n = len(cores)

    def helpers(s, d):
        src, dst = cores[s], cores[d]
        cand = [c for c in range(N_CORES)
                if topo.chip(c) == topo.chip(src) and c != src and topo.may_write(c, dst)]
        same = [c for c in cand if topo.die(c) == topo.die(src)]
        other = [c for c in cand if topo.die(c) != topo.die(src)]
        return [same[0], other[0], same[1], other[1]]

    out = []
    for s in range(1, n - 1):
        far = [d for d in range(s + 1, n) if not topo.may_write(cores[s], cores[d])]
        near = [d for d in range(s + 1, n) if topo.may_write(cores[s], cores[d])]
        for k, d in enumerate(far):
            out.append(dict(s=s, d=d, buf="in%d" % s, via=helpers(s, d)[k], land="drel", hsem="rel", hcnt=E_ON))
        for d in near:
            out.append(dict(s=s, d=d, buf="in%d" % s, via=None))
    far = [d for d in range(1, n) if not topo.may_write(cores[0], cores[d])]
    near = [d for d in range(1, n) if topo.may_write(cores[0], cores[d])]
    raw_to = far[-1]
    two = helpers(0, raw_to)[:2]
    out.append(dict(s=0, d=raw_to, buf="in0", via=two[0], land="drel", hsem="rel", hcnt=E_ON // 2))
    out.append(dict(s=0, d=raw_to, buf="inx", via=two[1], land="drel", hsem="rel", hcnt=E_ON // 2))
    for h, d in zip(two, far[-2::-1]):
        out.append(dict(s=0, d=d, buf="inp", via=h, land="prel", hsem="relp", hcnt=E_ON))
    for d in near:
        out.append(dict(s=0, d=d, buf="inp", via=None))
    return out


def _fan(topo, core, dsts, src, dst_ap, rsem, n_eng, skip=0):
    mask = topo.mask(core, dsts[0])
    for c in dsts[1:]:
        mask &= topo.mask(core, c)
    ids = []
    for c in dsts:
        rid, pid, _se = topo.addr(c)
        ids.append(DstId(rid=rid, pnc=pid))
    return RemoteDMATransfer(dst_ids=ids, dma_engine_mask=_bits(mask, n_eng, skip), remote_sem=rsem,
                             srcs=[src], dsts=[dst_ap for _c in dsts])


def rank_program(g, core, T, topo):
    R = _routes(T, topo)
    sem = T.sem
    cores = T.cores
    rank = T.rank_of(core)

    if rank is None:
        jobs = [r for r in R if r["via"] == core]
        for j in jobs:
            dst = cores[j["d"]]
            rid, pid, _se = topo.addr(dst)
            g.wait_ge(sem[j["hsem"]], j["hcnt"])
            g.remote_dma(out_ap=T[j["buf"]][:], in_ap=T[j["land"]][:], remote_sem=sem[ARR[j["buf"]]],
                         local_sem=sem.sent, pid=pid, routing_id=rid,
                         dma_engine_mask=_bits(topo.mask(core, dst), E_OFF))
        if jobs:
            g.wait_ge(sem.sent, E_OFF * len(jobs))
        return

    mine = [r for r in R if r["s"] == rank]
    n_lds = 16

    if rank == 0:
        g.sync.dma_start(T.dsend[0], T.m[:]).then_inc(sem.ldd, 16)
        g.scalar.dma_start(T.dsend[1], T.x[:]).then_inc(sem.ldd, 16)
        g.sync.dma_start(T.own[:], T.m[:]).then_inc(sem.lds, 16)
        g.scalar.dma_start(T.sx[:], T.x[:]).then_inc(sem.lds, 16)
        n_lds = 32
    else:
        if rank in STAGE:
            g.sync.dma_start(T.dsend[0], T[STAGE[rank]][:]).then_inc(sem.ldd, 16)
        g.sync.dma_start(T.own[:], T.m[:]).then_inc(sem.lds, 16)

    sent = 0
    if rank == 0:
        raw = [r for r in mine if r["land" if r["via"] is not None else "buf"] == "drel"]
        g.wait_ge(sem.ldd, 32)
        half = E_ON // 2
        g.remote_dma_fused([_fan(topo, core, [r["via"]], T.dsend[i], T.drel[:], sem.rel, half, skip=i * half)
                            for i, r in enumerate(raw)], local_sem=sem.sent)
        sent += half * len(raw)
        g.wait_ge(sem.cp0, 1)
        hp = [r["via"] for r in mine if r["buf"] == "inp" and r["via"] is not None]
        g.remote_dma_fused([_fan(topo, core, hp, T.t0[:], T.prel[:], sem.relp, E_ON)], local_sem=sem.sent)
        sent += E_ON
        near = sorted([r["d"] for r in mine if r["via"] is None], reverse=True)
        g.remote_dma_fused([_fan(topo, core, [cores[d] for d in near], T.t0[:], T.inp[:], sem.ap, E_OFF)],
                           local_sem=sem.sent)
        sent += E_OFF
    elif mine:
        buf = "in%d" % rank
        g.wait_ge(sem.ldd, 16)
        far = sorted([r for r in mine if r["via"] is not None], key=lambda r: -r["d"])
        g.remote_dma_fused([_fan(topo, core, [r["via"] for r in far], T.dsend[0], T.drel[:], sem.rel, E_ON)],
                           local_sem=sem.sent)
        sent += E_ON
        near = sorted([r["d"] for r in mine if r["via"] is None], reverse=True)
        if near:
            g.remote_dma_fused([_fan(topo, core, [cores[d] for d in near], T.dsend[0], T[buf][:], sem[ARR[buf]],
                                     E_OFF)], local_sem=sem.sent)
            sent += E_OFF

    waited = set()
    plan = PLAN[rank]
    for i, ops in enumerate(plan):
        for o in ops:
            if o in ("own", "sx"):
                w = ("lds", n_lds)
            elif o in ARR:
                w = (ARR[o], E_OFF)
            else:
                w = ("cp" + o[1:], 1)
            if w not in waited:
                waited.add(w)
                g.tensor.wait_ge(sem[w[0]], w[1])
        ps = T["ps%d" % i][:, 0:128]
        g.tensor.matmul(ps, T[ops[0]][:], T[ops[1]][:], start=True, stop=True).then_inc(sem["mm%d" % i], 1)
        g.vector.wait_ge(sem["mm%d" % i], 1)
        g.vector.tensor_copy(out=T["t%d" % i][:], in_=ps).then_inc(sem["cp%d" % i], 1)

    last = len(plan) - 1
    g.sync.wait_ge(sem["cp%d" % last], 1)
    g.sync.dma_start(T.y[:], T["t%d" % last][:]).then_inc(sem.st, 16)
    g.sync.wait_ge(sem.st, 16)
    if sent:
        g.wait_ge(sem.sent, sent)
